import numpy as np
import ml_dtypes


def mxq(x, axis, fmt="e4m3"):
    dtype, down = {"e4m3": (ml_dtypes.float8_e4m3fn, 7), "e5m2": (ml_dtypes.float8_e5m2, 14)}[fmt]
    v = np.moveaxis(np.asarray(x, np.float32).astype(ml_dtypes.bfloat16).astype(np.float64), axis, -1)
    blocks = v.reshape(v.shape[:-1] + (-1, 32))
    amax = np.abs(blocks).max(-1, keepdims=True)
    byte = np.maximum(np.where(amax > 0, np.frexp(amax)[1] - 1 + 127, 0) - down, 1)
    scale = np.exp2(byte - 127.0)
    codes = (blocks / scale).astype(np.float32).astype(dtype).astype(np.float64)
    return np.moveaxis((codes * scale).reshape(v.shape), -1, axis)


WIDE = False


def mx_kscale(k):
    if not WIDE:
        return np.ones(k)
    levels = np.array([10, -10, 5, -5, 0])
    if k % 512:
        return np.exp2(np.random.permutation(np.resize(levels, k // 32))).repeat(32)
    a = np.empty((k // 512, 16))
    for p in range(k // 512):
        a[p, :8] = np.random.permutation(np.resize(levels, 8))
        for g in range(8):
            far = levels[np.abs(levels - a[p, g]) >= 10]
            a[p, g + 8] = far[np.random.randint(len(far))]
    return np.exp2(a.ravel()).repeat(32)


def f64(x):
    return np.asarray(x).astype(np.float64)


def striped(idx):
    return np.tile(idx.reshape(-1, 16).T, (8, 1)).astype(np.uint16)


def unstriped(offs):
    return offs[:16].T.reshape(-1).astype(np.int64)


def pack_weight(w):
    k, n = w.shape
    w = f64(np.asarray(w, np.float32).astype(ml_dtypes.bfloat16)).reshape(k // 32, 32, n)
    amax = np.abs(w).max(1)
    byte = np.clip(np.where(amax > 0, np.frexp(amax)[1] - 1 + 127 - 7, 1), 1, 254)
    scaled = (w * np.exp2(127.0 - byte)[:, None, :]).reshape(k, n).astype(np.float32)
    words = np.ascontiguousarray(scaled.reshape(k // 512, 128, 4, n).transpose(0, 1, 3, 2)).astype(ml_dtypes.float8_e4m3fn).view(np.uint8)
    return words, np.ascontiguousarray(byte.astype(np.uint8).reshape(k // 512, 16, n))


def unpack_weight(words, scales):
    g, p, n, _ = words.shape
    vals = np.ascontiguousarray(words).view(ml_dtypes.float8_e4m3fn).astype(np.float64) * np.repeat(np.exp2(scales.astype(np.float64) - 127.0), 8, axis=1)[..., None]
    return vals.transpose(0, 1, 3, 2).reshape(g * 512, n)


def relu(v):
    return np.maximum(v, 0.0)


def sigmoid(v):
    return 1.0 / (1.0 + np.exp(-np.maximum(v, -700.0)))


K, T, S, H, N, R = 1024, 1024, 512, 512, 128, 1024


def setup_inputs():
    n = np.random.standard_normal
    s = mx_kscale(K)[:, None]
    u = mx_kscale(H)
    packed_xT = pack_weight(n((K, T)) * s)
    return {
        "x_words": packed_xT[0],
        "x_scales": packed_xT[1],
        "w1": (n((K, H)) / np.sqrt(K) / s * u).astype(np.float32),
        "w2": (n((H, N)) / np.sqrt(H) / u[:, None]).astype(np.float32),
        "wide": (0.5 * n((N, R))).astype(np.float32),
        "offs": striped(np.random.permutation(T)[:S]),
        "cross1": striped(np.random.randint(0, R, S)),
        "cross2": striped(np.random.randint(0, R, S)),
    }


def reference(x_words, x_scales, w1, w2, wide, offs, cross1, cross2):
    xq = unpack_weight(x_words, x_scales)[:, unstriped(offs)]
    h = relu(mxq(f64(w1), 0, "e4m3").T @ xq)
    y = mxq(f64(w2), 0, "e4m3").T @ mxq(h, 0, "e4m3")
    return sigmoid(y + f64(wide)[:, unstriped(cross1)] + f64(wide)[:, unstriped(cross2)])

@@ -1,0 +1,162 @@
+from contextlib import ExitStack
+
+import concourse.mybir as mybir
+
+K, T, S, H, N, R = 1024, 1024, 512, 512, 128, 1024
+FLOPS = 2 * K * H * S + 2 * H * N * S
+
+F32 = mybir.dt.float32
+BF16 = mybir.dt.bfloat16
+I32 = mybir.dt.int32
+U32 = mybir.dt.uint32
+U16 = mybir.dt.uint16
+U8 = mybir.dt.uint8
+FP8X4 = mybir.dt.float8_e4m3fn_x4
+ACT = mybir.ActivationFunctionType
+ADD = mybir.AluOpType.add
+
+P = 128
+PACK = 4
+PASSES = K // (P * PACK)
+CHUNK = 128
+CHUNKS = S // CHUNK
+LIST_COLS = CHUNK // 16
+M_SCALAR = 48
+
+
+def tile_picked_ywide_sigmoid_p_kernel(tc, x_words, x_scales, w1, w2, wide, offs, cross1, cross2, out):
+    nc = tc.nc
+    with ExitStack() as ctx:
+        keep = ctx.enter_context(tc.tile_pool(name="keep", bufs=1))
+        psum = ctx.enter_context(tc.psum_pool(name="psum", bufs=1))
+
+        def sb(name, shape, dtype):
+            return keep.tile(shape, dtype, name=name, align_bytes=64)
+
+        offs_sb = sb("offs_sb", [P, S // 16], U16)
+        cross1_sb = sb("cross1_sb", [P, S // 16], U16)
+        cross2_sb = sb("cross2_sb", [P, S // 16], U16)
+        scale_table = sb("scale_table", [P, T], U8)
+        word_table = [sb("word_table%d" % o, [P, T], I32) for o in range(PASSES)]
+        w1_raw = [sb("w1_raw%d" % o, [P, PACK, H], F32) for o in range(PASSES)]
+        w2_raw = sb("w2_raw", [P, PACK, N], F32)
+        wide_sb = sb("wide_sb", [P, R], F32)
+        warm_in = sb("warm_in", [P, 1], F32)
+        warm_out = sb("warm_out", [P, 1], F32)
+
+        nc.vector.memset(scale_table[:].bitcast(I32), 0)
+        nc.vector.memset(warm_in[:], 0.0)
+
+        def load_w1(o):
+            rows = w1[o * P * PACK : (o + 1) * P * PACK, :]
+            nc.sync.dma_start(out=w1_raw[o][:], in_=rows.rearrange("(p j) c -> p j c", j=PACK))
+
+        def load_words(o):
+            nc.sync.dma_start(out=word_table[o][:], in_=x_words[o].rearrange("p n t -> p (n t)").bitcast(I32))
+
+        nc.sync.dma_start(offs_sb[:], offs)
+        for q in range(4):
+            nc.scalar.dma_start(
+                out=scale_table[32 * q : 32 * q + 4 * PASSES, :].bitcast(I32),
+                in_=x_scales[:, 4 * q : 4 * q + 4, :].bitcast(I32),
+            )
+        nc.scalar.activation(warm_out[:], warm_in[:], ACT.Sigmoid)
+        load_w1(0)
+        load_words(0)
+        load_words(1)
+        load_w1(1)
+        nc.sync.dma_start(out=wide_sb[:], in_=wide)
+        nc.sync.dma_start(cross1_sb[:], cross1)
+        nc.sync.dma_start(cross2_sb[:], cross2)
+        nc.sync.dma_start(out=w2_raw[:], in_=w2.rearrange("(p j) n -> p j n", j=PACK))
+
+        x_scale = sb("x_scale", [P, S], U8)
+        x_code = [sb("x_code%d" % o, [P, S], U32) for o in range(PASSES)]
+        w1_bf = [sb("w1_bf%d" % o, [P, PACK, P, PACK], BF16) for o in range(PASSES)]
+        w1_code = [sb("w1_code%d" % o, [P, H], U32) for o in range(PASSES)]
+        w1_scale = [sb("w1_scale%d" % o, [P, H], U8) for o in range(PASSES)]
+
+        def cast_w1(o):
+            src = w1_raw[o][:].rearrange("p j (m t) -> p m j t", t=PACK)
+            dst = w1_bf[o][:].rearrange("p t m j -> p m j t")
+            nc.scalar.copy(dst[:, :M_SCALAR], src[:, :M_SCALAR])
+            nc.vector.tensor_copy(dst[:, M_SCALAR:], src[:, M_SCALAR:])
+
+        def quantize_w1(o, t0, t1):
+            cols = slice(t0 * P, t1 * P)
+            nc.vector.quantize_mx(
+                out=w1_code[o][:, cols].bitcast(FP8X4),
+                scales=w1_scale[o][:, cols],
+                in_=w1_bf[o][:, t0:t1].rearrange("p t m j -> p (t m j)"),
+            )
+
+        nc.vector.tensor_copy(x_scale[:], scale_table[:].indirect(offs_sb[:]))
+        cast_w1(0)
+        nc.vector.tensor_copy(x_code[0][:], word_table[0][:].bitcast(U32).indirect(offs_sb[:]))
+        quantize_w1(0, 0, PACK)
+        nc.vector.tensor_copy(x_code[1][:], word_table[1][:].bitcast(U32).indirect(offs_sb[:]))
+        cast_w1(1)
+        for t in range(PACK):
+            quantize_w1(1, t, t + 1)
+
+        w2_bf = sb("w2_bf", [P, N, PACK], BF16)
+        w2_code = sb("w2_code", [P, N], U32)
+        w2_scale = sb("w2_scale", [P, N], U8)
+        nc.scalar.copy(
+            w2_bf[:].rearrange("p (c i) j -> p c j i", i=4),
+            w2_raw[:].rearrange("p j (c i) -> p c j i", i=4),
+        )
+        wide1 = sb("wide1", [P, S], F32)
+        wide_sum = sb("wide_sum", [P, S], F32)
+        nc.vector.tensor_copy(wide1[:], wide_sb[:].indirect(cross1_sb[:]))
+        nc.vector.quantize_mx(
+            out=w2_code[:].bitcast(FP8X4), scales=w2_scale[:], in_=w2_bf[:].rearrange("p n j -> p (n j)")
+        )
+
+        h_bf, h_code, h_scale = [], [], []
+        for c in range(CHUNKS):
+            cols = slice(c * CHUNK, (c + 1) * CHUNK)
+            h_ps = psum.tile([P, PACK, CHUNK], F32, name="h_ps%d" % c)
+            for t in range(PACK):
+                m_cols = slice(t * P, (t + 1) * P)
+                for o in range(PASSES):
+                    nc.tensor.matmul_mx(
+                        out=h_ps[:, t, :],
+                        lhsT=w1_code[o][:, m_cols].bitcast(FP8X4),
+                        lhsT_scale=w1_scale[o][:, m_cols],
+                        rhs=x_code[o][:, cols].bitcast(FP8X4),
+                        rhs_scale=x_scale[4 * o : P, cols],
+                        start=(o == 0),
+                        stop=(o == PASSES - 1),
+                    )
+            h_bf.append(sb("h_bf%d" % c, [P, CHUNK, PACK], BF16))
+            h_code.append(sb("h_code%d" % c, [P, CHUNK], U32))
+            h_scale.append(sb("h_scale%d" % c, [P, CHUNK], U8))
+            nc.scalar.activation(h_bf[c][:], h_ps[:].rearrange("p t s -> p s t"), ACT.Relu)
+
+        for c in range(CHUNKS):
+            cols = slice(c * CHUNK, (c + 1) * CHUNK)
+            list_cols = slice(c * LIST_COLS, (c + 1) * LIST_COLS)
+            nc.vector.tensor_tensor(
+                wide_sum[:, cols], wide_sb[:].indirect(cross2_sb[:, list_cols]), wide1[:, cols], ADD
+            )
+            nc.vector.quantize_mx(
+                out=h_code[c][:].bitcast(FP8X4), scales=h_scale[c][:], in_=h_bf[c][:].rearrange("p s t -> p (s t)")
+            )
+        for c in range(CHUNKS):
+            cols = slice(c * CHUNK, (c + 1) * CHUNK)
+            y_ps = psum.tile([P, CHUNK], F32, name="y_ps%d" % c)
+            nc.tensor.matmul_mx(
+                out=y_ps[:],
+                lhsT=w2_code[:].bitcast(FP8X4),
+                lhsT_scale=w2_scale[:],
+                rhs=h_code[c][:].bitcast(FP8X4),
+                rhs_scale=h_scale[c][:],
+                start=True,
+                stop=True,
+            )
+            logit = sb("logit%d" % c, [P, CHUNK], F32)
+            result = sb("result%d" % c, [P, CHUNK], F32)
+            nc.vector.tensor_tensor(logit[:], y_ps[:], wide_sum[:, cols], ADD)
+            nc.scalar.activation(result[:], logit[:], ACT.Sigmoid)
+            nc.sync.dma_start(out=out[:, cols], in_=result[:])

@@ -18,145 +18,179 @@ ADD = mybir.AluOpType.add
 P = 128
 PACK = 4
 PASSES = K // (P * PACK)
+QUADRANT = 32
+SCALE_ROWS = 4
+ENTRIES_PER_COLUMN = 16
 CHUNK = 128
 CHUNKS = S // CHUNK
-LIST_COLS = CHUNK // 16
-M_SCALAR = 48
+HALF = S // 2
+MX_ALIGN = 64
+SCALAR_COLUMNS = (72, 48)
+WARM_PASSES = 2
 
 
-def tile_picked_ywide_sigmoid_p_kernel(tc, x_words, x_scales, w1, w2, wide, offs, cross1, cross2, out):
+def tile_picked_ywide_sigmoid_p_kernel(
+    tc, x_words, x_scales, w1, w2, wide, offs, cross1, cross2, out
+):
     nc = tc.nc
     with ExitStack() as ctx:
-        keep = ctx.enter_context(tc.tile_pool(name="keep", bufs=1))
+        sbuf = ctx.enter_context(tc.tile_pool(name="sbuf", bufs=1))
         psum = ctx.enter_context(tc.psum_pool(name="psum", bufs=1))
 
-        def sb(name, shape, dtype):
-            return keep.tile(shape, dtype, name=name, align_bytes=64)
+        def sbuf_tile(name, shape, dtype, tag=None):
+            return sbuf.tile(shape, dtype, name=name, tag=tag or name, align_bytes=MX_ALIGN)
 
-        offs_sb = sb("offs_sb", [P, S // 16], U16)
-        cross1_sb = sb("cross1_sb", [P, S // 16], U16)
-        cross2_sb = sb("cross2_sb", [P, S // 16], U16)
-        scale_table = sb("scale_table", [P, T], U8)
-        word_table = [sb("word_table%d" % o, [P, T], I32) for o in range(PASSES)]
-        w1_raw = [sb("w1_raw%d" % o, [P, PACK, H], F32) for o in range(PASSES)]
-        w2_raw = sb("w2_raw", [P, PACK, N], F32)
-        wide_sb = sb("wide_sb", [P, R], F32)
-        warm_in = sb("warm_in", [P, 1], F32)
-        warm_out = sb("warm_out", [P, 1], F32)
+        def samples(c0, c1):
+            return slice(c0 * CHUNK, c1 * CHUNK)
 
-        nc.vector.memset(scale_table[:].bitcast(I32), 0)
+        def quantize(codes, scales, values):
+            nc.vector.quantize_mx(out=codes.bitcast(FP8X4), scales=scales, in_=values)
+
+        def product(result, lhs_codes, lhs_scales, rhs_codes, rhs_scales, start, stop):
+            nc.tensor.matmul_mx(
+                out=result,
+                lhsT=lhs_codes.bitcast(FP8X4),
+                lhsT_scale=lhs_scales,
+                rhs=rhs_codes.bitcast(FP8X4),
+                rhs_scale=rhs_scales,
+                start=start,
+                stop=stop,
+            )
+
+        offs_sb = sbuf_tile("offs_sb", [P, S // ENTRIES_PER_COLUMN], U16)
+        cross1_sb = sbuf_tile("cross1_sb", [P, S // ENTRIES_PER_COLUMN], U16)
+        cross2_sb = sbuf_tile("cross2_sb", [P, S // ENTRIES_PER_COLUMN], U16)
+        scale_table = sbuf_tile("scale_table", [P, T], U8)
+        word_table = [sbuf_tile("word_table%d" % o, [P, T], I32) for o in range(PASSES)]
+        w1_raw = [sbuf_tile("w1_raw%d" % o, [P, PACK, H], F32) for o in range(PASSES)]
+        w2_raw = sbuf_tile("w2_raw", [P, PACK, N], F32)
+        wide_sb = sbuf_tile("wide_sb", [P, R], F32)
+
+        nc.gpsimd.memset(scale_table[:].bitcast(I32), 0)
+
+        warm_in = sbuf_tile("warm_in", [P, 1], F32)
+        warm_out = sbuf_tile("warm_out", [P, 1], F32)
         nc.vector.memset(warm_in[:], 0.0)
+        nc.scalar.activation(warm_out[:], warm_in[:], ACT.Sigmoid)
+
+        def load_words(o):
+            nc.sync.dma_start(out=word_table[o][:], in_=x_words[o].rearrange("p n j -> p (n j)").bitcast(I32))
 
         def load_w1(o):
             rows = w1[o * P * PACK : (o + 1) * P * PACK, :]
             nc.sync.dma_start(out=w1_raw[o][:], in_=rows.rearrange("(p j) c -> p j c", j=PACK))
 
-        def load_words(o):
-            nc.sync.dma_start(out=word_table[o][:], in_=x_words[o].rearrange("p n t -> p (n t)").bitcast(I32))
-
-        nc.sync.dma_start(offs_sb[:], offs)
-        for q in range(4):
-            nc.scalar.dma_start(
-                out=scale_table[32 * q : 32 * q + 4 * PASSES, :].bitcast(I32),
-                in_=x_scales[:, 4 * q : 4 * q + 4, :].bitcast(I32),
-            )
-        nc.scalar.activation(warm_out[:], warm_in[:], ACT.Sigmoid)
-        load_w1(0)
         load_words(0)
-        load_words(1)
+        nc.sync.dma_start(offs_sb[:], offs)
+        for q in range(P // QUADRANT):
+            nc.sync.dma_start(
+                out=scale_table[QUADRANT * q : QUADRANT * q + SCALE_ROWS * PASSES, :].bitcast(I32),
+                in_=x_scales[:, SCALE_ROWS * q : SCALE_ROWS * (q + 1), :].bitcast(I32),
+            )
+        load_w1(0)
         load_w1(1)
+        load_words(1)
+        nc.sync.dma_start(out=w2_raw[:], in_=w2.rearrange("(p j) n -> p j n", j=PACK))
         nc.sync.dma_start(out=wide_sb[:], in_=wide)
         nc.sync.dma_start(cross1_sb[:], cross1)
         nc.sync.dma_start(cross2_sb[:], cross2)
-        nc.sync.dma_start(out=w2_raw[:], in_=w2.rearrange("(p j) n -> p j n", j=PACK))
 
-        x_scale = sb("x_scale", [P, S], U8)
-        x_code = [sb("x_code%d" % o, [P, S], U32) for o in range(PASSES)]
-        w1_bf = [sb("w1_bf%d" % o, [P, PACK, P, PACK], BF16) for o in range(PASSES)]
-        w1_code = [sb("w1_code%d" % o, [P, H], U32) for o in range(PASSES)]
-        w1_scale = [sb("w1_scale%d" % o, [P, H], U8) for o in range(PASSES)]
+        x_scales_picked = sbuf_tile("x_scales_picked", [P, S], U8)
+        x_codes = [sbuf_tile("x_codes%d" % o, [P, S], U32) for o in range(PASSES)]
+        w1_bf = [sbuf_tile("w1_bf%d" % o, [P, PACK, P, PACK], BF16) for o in range(PASSES)]
+        w1_codes = [sbuf_tile("w1_codes%d" % o, [P, H], U32) for o in range(PASSES)]
+        w1_scales = [sbuf_tile("w1_scales%d" % o, [P, H], U8) for o in range(PASSES)]
+        w2_bf = sbuf_tile("w2_bf", [P, N, PACK], BF16)
+        w2_codes = sbuf_tile("w2_codes", [P, N], U32)
+        w2_scales = sbuf_tile("w2_scales", [P, N], U8)
+        h_bf = [sbuf_tile("h_bf%d" % u, [P, HALF, PACK], BF16) for u in range(2)]
+        h_codes = [sbuf_tile("h_codes%d" % u, [P, HALF], U32) for u in range(2)]
+        h_scales = [sbuf_tile("h_scales%d" % u, [P, HALF], U8) for u in range(2)]
+        wide_first = sbuf_tile("wide_first", [P, S], F32)
+        wide_sum = sbuf_tile("wide_sum", [P, S], F32)
+        result = sbuf_tile("result", [P, S], F32)
+        y_ps = [psum.tile([P, HALF], F32, name="y_ps%d" % u) for u in range(2)]
+        h_ps = [psum.tile([P, PACK, CHUNK], F32, name="h_ps%d" % c) for c in range(CHUNKS)]
 
-        def cast_w1(o):
+        def gather_words(o, c0, c1):
+            entries = offs_sb[:, c0 * CHUNK // ENTRIES_PER_COLUMN : c1 * CHUNK // ENTRIES_PER_COLUMN]
+            nc.vector.tensor_copy(x_codes[o][:, samples(c0, c1)], word_table[o][:].bitcast(U32).indirect(entries))
+
+        def quantize_w1(o):
             src = w1_raw[o][:].rearrange("p j (m t) -> p m j t", t=PACK)
             dst = w1_bf[o][:].rearrange("p t m j -> p m j t")
-            nc.scalar.copy(dst[:, :M_SCALAR], src[:, :M_SCALAR])
-            nc.vector.tensor_copy(dst[:, M_SCALAR:], src[:, M_SCALAR:])
+            split = SCALAR_COLUMNS[o]
+            nc.scalar.copy(dst[:, :split], src[:, :split])
+            nc.vector.tensor_copy(dst[:, split:], src[:, split:])
+            quantize(w1_codes[o][:], w1_scales[o][:], w1_bf[o][:].rearrange("p t m j -> p (t m j)"))
 
-        def quantize_w1(o, t0, t1):
-            cols = slice(t0 * P, t1 * P)
-            nc.vector.quantize_mx(
-                out=w1_code[o][:, cols].bitcast(FP8X4),
-                scales=w1_scale[o][:, cols],
-                in_=w1_bf[o][:, t0:t1].rearrange("p t m j -> p (t m j)"),
+        def first_product(c, t, o):
+            slot = slice(t * P, (t + 1) * P)
+            product(
+                h_ps[c][:, t, :],
+                w1_codes[o][:, slot],
+                w1_scales[o][:, slot],
+                x_codes[o][:, samples(c, c + 1)],
+                x_scales_picked[SCALE_ROWS * o : P, samples(c, c + 1)],
+                start=(o == 0),
+                stop=(o == PASSES - 1),
             )
 
-        nc.vector.tensor_copy(x_scale[:], scale_table[:].indirect(offs_sb[:]))
-        cast_w1(0)
-        nc.vector.tensor_copy(x_code[0][:], word_table[0][:].bitcast(U32).indirect(offs_sb[:]))
-        quantize_w1(0, 0, PACK)
-        nc.vector.tensor_copy(x_code[1][:], word_table[1][:].bitcast(U32).indirect(offs_sb[:]))
-        cast_w1(1)
-        for t in range(PACK):
-            quantize_w1(1, t, t + 1)
-
-        w2_bf = sb("w2_bf", [P, N, PACK], BF16)
-        w2_code = sb("w2_code", [P, N], U32)
-        w2_scale = sb("w2_scale", [P, N], U8)
-        nc.scalar.copy(
-            w2_bf[:].rearrange("p (c i) j -> p c j i", i=4),
-            w2_raw[:].rearrange("p j (c i) -> p c j i", i=4),
-        )
-        wide1 = sb("wide1", [P, S], F32)
-        wide_sum = sb("wide_sum", [P, S], F32)
-        nc.vector.tensor_copy(wide1[:], wide_sb[:].indirect(cross1_sb[:]))
-        nc.vector.quantize_mx(
-            out=w2_code[:].bitcast(FP8X4), scales=w2_scale[:], in_=w2_bf[:].rearrange("p n j -> p (n j)")
-        )
-
-        h_bf, h_code, h_scale = [], [], []
+        gather_words(0, 0, CHUNKS)
+        nc.vector.tensor_copy(x_scales_picked[:], scale_table[:].indirect(offs_sb[:]))
+        quantize_w1(0)
         for c in range(CHUNKS):
-            cols = slice(c * CHUNK, (c + 1) * CHUNK)
-            h_ps = psum.tile([P, PACK, CHUNK], F32, name="h_ps%d" % c)
-            for t in range(PACK):
-                m_cols = slice(t * P, (t + 1) * P)
-                for o in range(PASSES):
-                    nc.tensor.matmul_mx(
-                        out=h_ps[:, t, :],
-                        lhsT=w1_code[o][:, m_cols].bitcast(FP8X4),
-                        lhsT_scale=w1_scale[o][:, m_cols],
-                        rhs=x_code[o][:, cols].bitcast(FP8X4),
-                        rhs_scale=x_scale[4 * o : P, cols],
-                        start=(o == 0),
-                        stop=(o == PASSES - 1),
-                    )
-            h_bf.append(sb("h_bf%d" % c, [P, CHUNK, PACK], BF16))
-            h_code.append(sb("h_code%d" % c, [P, CHUNK], U32))
-            h_scale.append(sb("h_scale%d" % c, [P, CHUNK], U8))
-            nc.scalar.activation(h_bf[c][:], h_ps[:].rearrange("p t s -> p s t"), ACT.Relu)
+            first_product(c, 0, 0)
 
-        for c in range(CHUNKS):
-            cols = slice(c * CHUNK, (c + 1) * CHUNK)
-            list_cols = slice(c * LIST_COLS, (c + 1) * LIST_COLS)
-            nc.vector.tensor_tensor(
-                wide_sum[:, cols], wide_sb[:].indirect(cross2_sb[:, list_cols]), wide1[:, cols], ADD
-            )
-            nc.vector.quantize_mx(
-                out=h_code[c][:].bitcast(FP8X4), scales=h_scale[c][:], in_=h_bf[c][:].rearrange("p s t -> p (s t)")
-            )
-        for c in range(CHUNKS):
-            cols = slice(c * CHUNK, (c + 1) * CHUNK)
-            y_ps = psum.tile([P, CHUNK], F32, name="y_ps%d" % c)
-            nc.tensor.matmul_mx(
-                out=y_ps[:],
-                lhsT=w2_code[:].bitcast(FP8X4),
-                lhsT_scale=w2_scale[:],
-                rhs=h_code[c][:].bitcast(FP8X4),
-                rhs_scale=h_scale[c][:],
+        warm_ps = psum.tile([P, S], F32, name="warm_ps")
+        for t in range(WARM_PASSES):
+            slot = slice(t * P, (t + 1) * P)
+            product(
+                warm_ps[:],
+                w1_codes[0][:, slot],
+                w1_scales[0][:, slot],
+                x_codes[0][:],
+                x_scales_picked[:],
                 start=True,
                 stop=True,
             )
-            logit = sb("logit%d" % c, [P, CHUNK], F32)
-            result = sb("result%d" % c, [P, CHUNK], F32)
-            nc.vector.tensor_tensor(logit[:], y_ps[:], wide_sum[:, cols], ADD)
-            nc.scalar.activation(result[:], logit[:], ACT.Sigmoid)
-            nc.sync.dma_start(out=out[:, cols], in_=result[:])
+
+        quantize_w1(1)
+        nc.scalar.copy(
+            w2_bf[:].rearrange("p (c i) j -> p c j i", i=PACK),
+            w2_raw[:].rearrange("p j (c i) -> p c j i", i=PACK),
+        )
+        gather_words(1, 0, 1)
+        gather_words(1, 1, 2)
+        gather_words(1, 2, CHUNKS)
+        for c in range(CHUNKS):
+            first_product(c, 0, 1)
+            for t in range(1, PACK):
+                for o in range(PASSES):
+                    first_product(c, t, o)
+            u, place = divmod(c, CHUNKS // 2)
+            nc.scalar.activation(
+                h_bf[u][:, samples(place, place + 1), :], h_ps[c][:].rearrange("p t s -> p s t"), ACT.Relu
+            )
+
+        nc.vector.tensor_copy(wide_first[:], wide_sb[:].indirect(cross1_sb[:]))
+        quantize(w2_codes[:], w2_scales[:], w2_bf[:].rearrange("p n j -> p (n j)"))
+        nc.vector.tensor_tensor(wide_sum[:], wide_sb[:].indirect(cross2_sb[:]), wide_first[:], ADD)
+
+        for u in range(2):
+            quantize(h_codes[u][:], h_scales[u][:], h_bf[u][:].rearrange("p s t -> p (s t)"))
+            product(y_ps[u][:], w2_codes[:], w2_scales[:], h_codes[u][:], h_scales[u][:], start=True, stop=True)
+
+        logits = [sbuf_tile("logits%d" % u, [P, HALF], F32, tag="h_bf%d" % (1 - u)) for u in range(2)]
+
+        def finish(c0, c1):
+            u = c0 // (CHUNKS // 2)
+            in_half = samples(c0 - u * CHUNKS // 2, c1 - u * CHUNKS // 2)
+            nc.vector.tensor_tensor(logits[u][:, in_half], y_ps[u][:, in_half], wide_sum[:, samples(c0, c1)], ADD)
+            nc.scalar.activation(result[:, samples(c0, c1)], logits[u][:, in_half], ACT.Sigmoid)
+
+        finish(0, 2)
+        nc.sync.dma_start(out=out[:, :HALF], in_=result[:, :HALF])
+        finish(2, 3)
+        finish(3, 4)
+        nc.sync.dma_start(out=out[:, HALF:], in_=result[:, HALF:])

from contextlib import ExitStack

import concourse.mybir as mybir

K, T, S, H, N, R = 1024, 1024, 512, 512, 128, 1024
FLOPS = 2 * K * H * S + 2 * H * N * S

F32 = mybir.dt.float32
BF16 = mybir.dt.bfloat16
I32 = mybir.dt.int32
U32 = mybir.dt.uint32
U16 = mybir.dt.uint16
U8 = mybir.dt.uint8
FP8X4 = mybir.dt.float8_e4m3fn_x4
ACT = mybir.ActivationFunctionType
ADD = mybir.AluOpType.add

P = 128
PACK = 4
PASSES = K // (P * PACK)
QUADRANT = 32
SCALE_ROWS = 4
ENTRIES_PER_COLUMN = 16
CHUNK = 128
CHUNKS = S // CHUNK
HALF = S // 2
MX_ALIGN = 64
SCALAR_COLUMNS = (72, 48)
WARM_PASSES = 2


def tile_picked_ywide_sigmoid_p_kernel(
    tc, x_words, x_scales, w1, w2, wide, offs, cross1, cross2, out
):
    nc = tc.nc
    with ExitStack() as ctx:
        sbuf = ctx.enter_context(tc.tile_pool(name="sbuf", bufs=1))
        psum = ctx.enter_context(tc.psum_pool(name="psum", bufs=1))

        def sbuf_tile(name, shape, dtype, tag=None):
            return sbuf.tile(shape, dtype, name=name, tag=tag or name, align_bytes=MX_ALIGN)

        def samples(c0, c1):
            return slice(c0 * CHUNK, c1 * CHUNK)

        def quantize(codes, scales, values):
            nc.vector.quantize_mx(out=codes.bitcast(FP8X4), scales=scales, in_=values)

        def product(result, lhs_codes, lhs_scales, rhs_codes, rhs_scales, start, stop):
            nc.tensor.matmul_mx(
                out=result,
                lhsT=lhs_codes.bitcast(FP8X4),
                lhsT_scale=lhs_scales,
                rhs=rhs_codes.bitcast(FP8X4),
                rhs_scale=rhs_scales,
                start=start,
                stop=stop,
            )

        offs_sb = sbuf_tile("offs_sb", [P, S // ENTRIES_PER_COLUMN], U16)
        cross1_sb = sbuf_tile("cross1_sb", [P, S // ENTRIES_PER_COLUMN], U16)
        cross2_sb = sbuf_tile("cross2_sb", [P, S // ENTRIES_PER_COLUMN], U16)
        scale_table = sbuf_tile("scale_table", [P, T], U8)
        word_table = [sbuf_tile("word_table%d" % o, [P, T], I32) for o in range(PASSES)]
        w1_raw = [sbuf_tile("w1_raw%d" % o, [P, PACK, H], F32) for o in range(PASSES)]
        w2_raw = sbuf_tile("w2_raw", [P, PACK, N], F32)
        wide_sb = sbuf_tile("wide_sb", [P, R], F32)

        nc.gpsimd.memset(scale_table[:].bitcast(I32), 0)

        warm_in = sbuf_tile("warm_in", [P, 1], F32)
        warm_out = sbuf_tile("warm_out", [P, 1], F32)
        nc.vector.memset(warm_in[:], 0.0)
        nc.scalar.activation(warm_out[:], warm_in[:], ACT.Sigmoid)

        def load_words(o):
            nc.sync.dma_start(out=word_table[o][:], in_=x_words[o].rearrange("p n j -> p (n j)").bitcast(I32))

        def load_w1(o):
            rows = w1[o * P * PACK : (o + 1) * P * PACK, :]
            nc.sync.dma_start(out=w1_raw[o][:], in_=rows.rearrange("(p j) c -> p j c", j=PACK))

        load_words(0)
        nc.sync.dma_start(offs_sb[:], offs)
        for q in range(P // QUADRANT):
            nc.sync.dma_start(
                out=scale_table[QUADRANT * q : QUADRANT * q + SCALE_ROWS * PASSES, :].bitcast(I32),
                in_=x_scales[:, SCALE_ROWS * q : SCALE_ROWS * (q + 1), :].bitcast(I32),
            )
        load_w1(0)
        load_w1(1)
        load_words(1)
        nc.sync.dma_start(out=w2_raw[:], in_=w2.rearrange("(p j) n -> p j n", j=PACK))
        nc.sync.dma_start(out=wide_sb[:], in_=wide)
        nc.sync.dma_start(cross1_sb[:], cross1)
        nc.sync.dma_start(cross2_sb[:], cross2)

        x_scales_picked = sbuf_tile("x_scales_picked", [P, S], U8)
        x_codes = [sbuf_tile("x_codes%d" % o, [P, S], U32) for o in range(PASSES)]
        w1_bf = [sbuf_tile("w1_bf%d" % o, [P, PACK, P, PACK], BF16) for o in range(PASSES)]
        w1_codes = [sbuf_tile("w1_codes%d" % o, [P, H], U32) for o in range(PASSES)]
        w1_scales = [sbuf_tile("w1_scales%d" % o, [P, H], U8) for o in range(PASSES)]
        w2_bf = sbuf_tile("w2_bf", [P, N, PACK], BF16)
        w2_codes = sbuf_tile("w2_codes", [P, N], U32)
        w2_scales = sbuf_tile("w2_scales", [P, N], U8)
        h_bf = [sbuf_tile("h_bf%d" % u, [P, HALF, PACK], BF16) for u in range(2)]
        h_codes = [sbuf_tile("h_codes%d" % u, [P, HALF], U32) for u in range(2)]
        h_scales = [sbuf_tile("h_scales%d" % u, [P, HALF], U8) for u in range(2)]
        wide_first = sbuf_tile("wide_first", [P, S], F32)
        wide_sum = sbuf_tile("wide_sum", [P, S], F32)
        result = sbuf_tile("result", [P, S], F32)
        y_ps = [psum.tile([P, HALF], F32, name="y_ps%d" % u) for u in range(2)]
        h_ps = [psum.tile([P, PACK, CHUNK], F32, name="h_ps%d" % c) for c in range(CHUNKS)]

        def gather_words(o, c0, c1):
            entries = offs_sb[:, c0 * CHUNK // ENTRIES_PER_COLUMN : c1 * CHUNK // ENTRIES_PER_COLUMN]
            nc.vector.tensor_copy(x_codes[o][:, samples(c0, c1)], word_table[o][:].bitcast(U32).indirect(entries))

        def quantize_w1(o):
            src = w1_raw[o][:].rearrange("p j (m t) -> p m j t", t=PACK)
            dst = w1_bf[o][:].rearrange("p t m j -> p m j t")
            split = SCALAR_COLUMNS[o]
            nc.scalar.copy(dst[:, :split], src[:, :split])
            nc.vector.tensor_copy(dst[:, split:], src[:, split:])
            quantize(w1_codes[o][:], w1_scales[o][:], w1_bf[o][:].rearrange("p t m j -> p (t m j)"))

        def first_product(c, t, o):
            slot = slice(t * P, (t + 1) * P)
            product(
                h_ps[c][:, t, :],
                w1_codes[o][:, slot],
                w1_scales[o][:, slot],
                x_codes[o][:, samples(c, c + 1)],
                x_scales_picked[SCALE_ROWS * o : P, samples(c, c + 1)],
                start=(o == 0),
                stop=(o == PASSES - 1),
            )

        gather_words(0, 0, CHUNKS)
        nc.vector.tensor_copy(x_scales_picked[:], scale_table[:].indirect(offs_sb[:]))
        quantize_w1(0)
        for c in range(CHUNKS):
            first_product(c, 0, 0)

        warm_ps = psum.tile([P, S], F32, name="warm_ps")
        for t in range(WARM_PASSES):
            slot = slice(t * P, (t + 1) * P)
            product(
                warm_ps[:],
                w1_codes[0][:, slot],
                w1_scales[0][:, slot],
                x_codes[0][:],
                x_scales_picked[:],
                start=True,
                stop=True,
            )

        quantize_w1(1)
        nc.scalar.copy(
            w2_bf[:].rearrange("p (c i) j -> p c j i", i=PACK),
            w2_raw[:].rearrange("p j (c i) -> p c j i", i=PACK),
        )
        gather_words(1, 0, 1)
        gather_words(1, 1, 2)
        gather_words(1, 2, CHUNKS)
        for c in range(CHUNKS):
            first_product(c, 0, 1)
            for t in range(1, PACK):
                for o in range(PASSES):
                    first_product(c, t, o)
            u, place = divmod(c, CHUNKS // 2)
            nc.scalar.activation(
                h_bf[u][:, samples(place, place + 1), :], h_ps[c][:].rearrange("p t s -> p s t"), ACT.Relu
            )

        nc.vector.tensor_copy(wide_first[:], wide_sb[:].indirect(cross1_sb[:]))
        quantize(w2_codes[:], w2_scales[:], w2_bf[:].rearrange("p n j -> p (n j)"))
        nc.vector.tensor_tensor(wide_sum[:], wide_sb[:].indirect(cross2_sb[:]), wide_first[:], ADD)

        for u in range(2):
            quantize(h_codes[u][:], h_scales[u][:], h_bf[u][:].rearrange("p s t -> p (s t)"))
            product(y_ps[u][:], w2_codes[:], w2_scales[:], h_codes[u][:], h_scales[u][:], start=True, stop=True)

        logits = [sbuf_tile("logits%d" % u, [P, HALF], F32, tag="h_bf%d" % (1 - u)) for u in range(2)]

        def finish(c0, c1):
            u = c0 // (CHUNKS // 2)
            in_half = samples(c0 - u * CHUNKS // 2, c1 - u * CHUNKS // 2)
            nc.vector.tensor_tensor(logits[u][:, in_half], y_ps[u][:, in_half], wide_sum[:, samples(c0, c1)], ADD)
            nc.scalar.activation(result[:, samples(c0, c1)], logits[u][:, in_half], ACT.Sigmoid)

        finish(0, 2)
        nc.sync.dma_start(out=out[:, :HALF], in_=result[:, :HALF])
        finish(2, 3)
        finish(3, 4)
        nc.sync.dma_start(out=out[:, HALF:], in_=result[:, HALF:])
